import numpy as np
import ml_dtypes


def mxq(x, axis, fmt="e4m3"):
    dtype, down = {"e4m3": (ml_dtypes.float8_e4m3fn, 7), "e5m2": (ml_dtypes.float8_e5m2, 14)}[fmt]
    v = np.moveaxis(np.asarray(x, np.float32).astype(ml_dtypes.bfloat16).astype(np.float64), axis, -1)
    blocks = v.reshape(v.shape[:-1] + (-1, 32))
    amax = np.abs(blocks).max(-1, keepdims=True)
    byte = np.maximum(np.where(amax > 0, np.frexp(amax)[1] - 1 + 127, 0) - down, 1)
    scale = np.exp2(byte - 127.0)
    codes = (blocks / scale).astype(np.float32).astype(dtype).astype(np.float64)
    return np.moveaxis((codes * scale).reshape(v.shape), -1, axis)


WIDE = False


def mx_kscale(k):
    if not WIDE:
        return np.ones(k)
    levels = np.array([10, -10, 5, -5, 0])
    if k % 512:
        return np.exp2(np.random.permutation(np.resize(levels, k // 32))).repeat(32)
    a = np.empty((k // 512, 16))
    for p in range(k // 512):
        a[p, :8] = np.random.permutation(np.resize(levels, 8))
        for g in range(8):
            far = levels[np.abs(levels - a[p, g]) >= 10]
            a[p, g + 8] = far[np.random.randint(len(far))]
    return np.exp2(a.ravel()).repeat(32)


def f64(x):
    return np.asarray(x).astype(np.float64)


def striped(idx):
    return np.tile(idx.reshape(-1, 16).T, (8, 1)).astype(np.uint16)


def unstriped(offs):
    return offs[:16].T.reshape(-1).astype(np.int64)


def pack_weight(w):
    k, n = w.shape
    w = f64(np.asarray(w, np.float32).astype(ml_dtypes.bfloat16)).reshape(k // 32, 32, n)
    amax = np.abs(w).max(1)
    byte = np.clip(np.where(amax > 0, np.frexp(amax)[1] - 1 + 127 - 7, 1), 1, 254)
    scaled = (w * np.exp2(127.0 - byte)[:, None, :]).reshape(k, n).astype(np.float32)
    words = np.ascontiguousarray(scaled.reshape(k // 512, 128, 4, n).transpose(0, 1, 3, 2)).astype(ml_dtypes.float8_e4m3fn).view(np.uint8)
    return words, np.ascontiguousarray(byte.astype(np.uint8).reshape(k // 512, 16, n))


def unpack_weight(words, scales):
    g, p, n, _ = words.shape
    vals = np.ascontiguousarray(words).view(ml_dtypes.float8_e4m3fn).astype(np.float64) * np.repeat(np.exp2(scales.astype(np.float64) - 127.0), 8, axis=1)[..., None]
    return vals.transpose(0, 1, 3, 2).reshape(g * 512, n)


def sigmoid(v):
    return 1.0 / (1.0 + np.exp(-np.maximum(v, -700.0)))


K, T, S, V = 1024, 2048, 512, 256
P = 2 ** 7


def setup_inputs():
    n = np.random.standard_normal
    s = mx_kscale(K)[:, None]
    packed_xT = pack_weight(n((K, T)) * s)
    return {
        "x_words": packed_xT[0],
        "x_scales": packed_xT[1],
        "hT": (n((K, V)) / np.sqrt(K) / s).astype(np.float32),
        "nn": (np.tile(np.random.uniform(3.0, 4.0, T), (P, 1))).astype(np.float32),
        "own": (np.random.uniform(2.0, 3.0, (V, 1))).astype(np.float32),
        "depot": (np.tile(np.random.uniform(0.5, 3.0, T), (P, 1))).astype(np.float32),
        "dep2": (np.random.uniform(0.5, 3.0, (V, 1))).astype(np.float32),
        "dem": (np.tile(np.random.uniform(0.1, 0.8, T), (P, 1))).astype(np.float32),
        "load": (np.random.uniform(0.1, 0.7, (V, 1))).astype(np.float32),
        "offs": striped(np.random.permutation(T)[:S]),
    }


def reference(x_words, x_scales, hT, nn, own, depot, dep2, dem, load, offs):
    hTq = mxq(f64(hT), 0, "e4m3")
    xq = unpack_weight(x_words, x_scales)[:, unstriped(offs)]
    y = 0.6 * (hTq.T @ xq)
    dist = np.sqrt(f64(nn)[:1][:, unstriped(offs)] - y + f64(own))
    sav = f64(depot)[:1][:, unstriped(offs)] - (1.2 * dist) + f64(dep2)
    ld = f64(dem)[:1][:, unstriped(offs)] + f64(load)
    return sav * (sigmoid(-8.0 * (ld - 1.0)))

@@ -1,0 +1,178 @@
+from contextlib import ExitStack
+
+import concourse.mybir as mybir
+from concourse.masks import make_identity
+
+K, T, S, V = 1024, 2048, 512, 256
+FLOPS = 2 * K * S * V
+BYTES = K * T + K * T // 32 + 4 * K * V + 3 * 4 * T + 3 * 4 * V + 2 * 128 * S // 16 + 4 * V * S
+
+F32 = mybir.dt.float32
+BF16 = mybir.dt.bfloat16
+U32 = mybir.dt.uint32
+I32 = mybir.dt.int32
+U16 = mybir.dt.uint16
+U8 = mybir.dt.uint8
+FP8X4 = mybir.dt.float8_e4m3fn_x4
+ACT = mybir.ActivationFunctionType
+ALU = mybir.AluOpType
+
+P = 128
+PACK = 4
+PASSES = K // (P * PACK)
+ROUTE_TILES = V // P
+HALF = S // 2
+ROW0, ROW_STEP = 8, 4
+
+
+def tile_picked_ysavcw_feas_p_kernel(
+    tc, x_words, x_scales, hT, nn, own, depot, dep2, dem, load, offs, out
+):
+    nc = tc.nc
+    with ExitStack() as ctx:
+        sb = ctx.enter_context(tc.tile_pool(name="sb", bufs=1))
+        ps = ctx.enter_context(tc.psum_pool(name="ps", bufs=1))
+
+        offsets = sb.tile([P, S // 16], U16, name="offsets")
+        nc.sync.dma_start(offsets[:], offs)
+
+        cols = {}
+        for name, src in (("load", load), ("own", own), ("dep2", dep2)):
+            cols[name] = sb.tile([P, ROUTE_TILES], F32, name=name + "_col")
+            with nc.allow_non_contiguous_dma(reason="one value a partition"):
+                nc.scalar.dma_start(cols[name][:], src.rearrange("(c p) one -> p (c one)", p=P))
+
+        tables = sb.tile([P, T], F32, name="tables")
+        nc.vector.memset(tables[:], 0.0)
+        for r, src in enumerate((dem, nn, depot)):
+            row = ROW0 + ROW_STEP * r
+            nc.scalar.dma_start(tables[row : row + 1, :], src[0:1, :])
+
+        planes = sb.tile([P, T], U8, name="planes", tag="planes", align_bytes=64)
+        nc.vector.memset(planes[:].bitcast(I32), 0)
+        ident = sb.tile([P, P], F32, name="ident")
+        make_identity(nc, ident[:])
+        for q in range(4):
+            nc.gpsimd.dma_start(
+                planes[32 * q : 32 * q + 4 * PASSES, :].bitcast(I32),
+                x_scales[:, 4 * q : 4 * q + 4, :].bitcast(I32),
+            )
+
+        h_raw = []
+        for o in range(PASSES):
+            raw = sb.tile([P, PACK, V], F32, name=f"h_raw{o}", tag=f"stage{o}", align_bytes=64)
+            nc.sync.dma_start(raw[:], hT[o * P * PACK : (o + 1) * P * PACK, :].rearrange("(p j) t -> p j t", j=PACK))
+            h_raw.append(raw)
+        words = []
+
+        def load_words(o, tag):
+            w = sb.tile([P, T], U32, name=f"words{o}", tag=tag, align_bytes=64)
+            nc.sync.dma_start(w[:].bitcast(I32), x_words[o].rearrange("p n r -> p (n r)").bitcast(I32))
+            words.append(w)
+
+        load_words(0, "words0")
+
+        h_bf, h_codes, h_scales = [], [], []
+        for o in range(PASSES):
+            g = sb.tile([P, V, PACK], BF16, name=f"h_bf{o}", align_bytes=64)
+            nc.vector.tensor_copy(
+                out=g[:].rearrange("p (c i) j -> p c j i", i=4),
+                in_=h_raw[o][:].rearrange("p j (c i) -> p c j i", i=4),
+            )
+            h_bf.append(g)
+        load_words(1, "stage0")
+        for o in range(PASSES):
+            codes = sb.tile([P, V], U32, name=f"h_codes{o}", align_bytes=64)
+            scales = sb.tile([P, V], U8, name=f"h_scales{o}", align_bytes=64)
+            nc.vector.quantize_mx(out=codes[:].bitcast(FP8X4), scales=scales[:], in_=h_bf[o][:].rearrange("p t j -> p (t j)"))
+            h_codes.append(codes)
+            h_scales.append(scales)
+
+        gate_bias = sb.tile([P, ROUTE_TILES], F32, name="gate_bias")
+        nc.vector.tensor_scalar(gate_bias[:], cols["load"][:], -4.0, 4.0, ALU.mult, ALU.add)
+        root_bias = sb.tile([P, ROUTE_TILES], F32, name="root_bias")
+        nc.vector.tensor_scalar(root_bias[:], cols["own"][:], 0.36, None, ALU.mult)
+        half_dep2 = sb.tile([P, ROUTE_TILES], F32, name="half_dep2")
+        nc.vector.tensor_scalar(half_dep2[:], cols["dep2"][:], 0.5, None, ALU.mult)
+
+        picked = sb.tile([P, S], F32, name="picked")
+        nc.scalar.activation(picked[:], tables[:].indirect(offsets[:]), ACT.Copy)
+        columns = sb.tile([P, S // P, 3], F32, name="columns")
+        for a in range(2):
+            turned = ps.tile([P, 2, P], F32, name=f"turned{a}", tag=f"acc{a}")
+            for i in range(2):
+                b = 2 * a + i
+                nc.tensor.transpose(turned[:, i, :], picked[:, b * P : (b + 1) * P], ident[:])
+            nc.scalar.activation(
+                columns[:, 2 * a : 2 * a + 2, :], turned[:, :, ROW0 : ROW0 + 2 * ROW_STEP + 1 : ROW_STEP], ACT.Copy, scale=0.5
+            )
+        spread = []
+        for r in range(3):
+            bank = ps.tile([P, S], F32, name=f"spread{r}", tag=f"bank{r}")
+            for b in range(S // P):
+                nc.tensor.transpose(bank[:, b * P : (b + 1) * P], columns[:, b, r : r + 1].to_broadcast([P, P]), ident[:])
+            spread.append(bank)
+        dem_rows, nn_bank, depot_rows = spread
+        gate = []
+        for c in range(ROUTE_TILES):
+            gt = sb.tile([P, S], F32, name=f"gate{c}")
+            nc.scalar.activation(gt[:], dem_rows[:], ACT.Tanh, bias=gate_bias[:, c : c + 1], scale=-8.0)
+            gate.append(gt)
+        nn_rows = sb.tile([P, S], F32, name="nn_rows")
+        nc.scalar.copy(nn_rows[:], nn_bank[:])
+
+        x_sc = sb.tile([P, S], U8, name="x_sc", align_bytes=64)
+        nc.vector.tensor_copy(x_sc[:], planes[:].indirect(offsets[:]))
+        x0 = sb.tile([P, S], U32, name="x0", align_bytes=64)
+        nc.vector.tensor_copy(x0[:], words[0][:].indirect(offsets[:]))
+        x1 = []
+        for a in range(2):
+            xt = sb.tile([P, HALF], U32, name=f"x1_{a}", tag=("planes", "x1")[a], align_bytes=64)
+            nc.vector.tensor_copy(xt[:], words[1][:].indirect(offsets[:, a * HALF // 16 : (a + 1) * HALF // 16]))
+            x1.append(xt)
+
+        quarters = [(a, c) for a in range(2) for c in range(ROUTE_TILES)]
+        acc = {}
+        for a, c in quarters:
+            acc[a, c] = ps.tile([P, HALF], F32, name=f"acc{a}{c}", tag=f"bank{c}" if a else f"acc{c}")
+        for o in range(PASSES):
+            for a, c in quarters:
+                js = slice(a * HALF, (a + 1) * HALF)
+                ts = slice(c * P, (c + 1) * P)
+                rhs = x0[:, js] if o == 0 else x1[a][:]
+                nc.tensor.matmul_mx(
+                    out=acc[a, c][:],
+                    lhsT=h_codes[o][:, ts].bitcast(FP8X4),
+                    lhsT_scale=h_scales[o][:, ts],
+                    rhs=rhs.bitcast(FP8X4),
+                    rhs_scale=x_sc[4 * o : P, js],
+                    start=(o == 0),
+                    stop=(o == PASSES - 1),
+                )
+
+        root, sav = {}, {}
+
+        def distance(a, c):
+            js = slice(a * HALF, (a + 1) * HALF)
+            u = sb.tile([P, HALF], F32, name=f"u{a}{c}")
+            nc.vector.scalar_tensor_tensor(u[:], acc[a, c][:], -0.3, nn_rows[:, js], ALU.mult, ALU.add)
+            root[a, c] = sb.tile([P, HALF], F32, name=f"root{a}{c}")
+            nc.scalar.activation(root[a, c][:], u[:], ACT.Sqrt, bias=root_bias[:, c : c + 1], scale=0.72)
+
+        def saving(a, c):
+            js = slice(a * HALF, (a + 1) * HALF)
+            sav[a, c] = sb.tile([P, HALF], F32, name=f"sav{a}{c}")
+            nc.vector.scalar_tensor_tensor(
+                sav[a, c][:], depot_rows[:, js], half_dep2[:, c : c + 1], root[a, c][:], ALU.add, ALU.subtract
+            )
+
+        def result(a, c):
+            js = slice(a * HALF, (a + 1) * HALF)
+            res = sb.tile([P, HALF], F32, name=f"res{a}{c}")
+            nc.vector.scalar_tensor_tensor(res[:], gate[c][:, js], 1.0, sav[a, c][:], ALU.add, ALU.mult)
+            nc.sync.dma_start(out[c * P : (c + 1) * P, js], res[:])
+
+        for step in range(len(quarters) + 3):
+            for stage, lag in ((distance, 0), (saving, 2), (result, 3)):
+                if 0 <= step - lag < len(quarters):
+                    stage(*quarters[step - lag])

@@ -22,7 +22,8 @@ PACK = 4
 PASSES = K // (P * PACK)
 ROUTE_TILES = V // P
 HALF = S // 2
-ROW0, ROW_STEP = 8, 4
+BLOCKS = S // P
+ROW0 = P - 3
 
 
 def tile_picked_ysavcw_feas_p_kernel(
@@ -36,33 +37,17 @@ def tile_picked_ysavcw_feas_p_kernel(
         offsets = sb.tile([P, S // 16], U16, name="offsets")
         nc.sync.dma_start(offsets[:], offs)
 
-        cols = {}
-        for name, src in (("load", load), ("own", own), ("dep2", dep2)):
-            cols[name] = sb.tile([P, ROUTE_TILES], F32, name=name + "_col")
+        def load_column(name, src, queue):
+            col = sb.tile([P, ROUTE_TILES], F32, name=name)
             with nc.allow_non_contiguous_dma(reason="one value a partition"):
-                nc.scalar.dma_start(cols[name][:], src.rearrange("(c p) one -> p (c one)", p=P))
+                queue.dma_start(col[:], src.rearrange("(c p) one -> p (c one)", p=P))
+            return col
 
-        tables = sb.tile([P, T], F32, name="tables")
-        nc.vector.memset(tables[:], 0.0)
-        for r, src in enumerate((dem, nn, depot)):
-            row = ROW0 + ROW_STEP * r
-            nc.scalar.dma_start(tables[row : row + 1, :], src[0:1, :])
-
-        planes = sb.tile([P, T], U8, name="planes", tag="planes", align_bytes=64)
-        nc.vector.memset(planes[:].bitcast(I32), 0)
-        ident = sb.tile([P, P], F32, name="ident")
-        make_identity(nc, ident[:])
-        for q in range(4):
-            nc.gpsimd.dma_start(
-                planes[32 * q : 32 * q + 4 * PASSES, :].bitcast(I32),
-                x_scales[:, 4 * q : 4 * q + 4, :].bitcast(I32),
-            )
-
-        h_raw = []
-        for o in range(PASSES):
+        def load_h(o):
             raw = sb.tile([P, PACK, V], F32, name=f"h_raw{o}", tag=f"stage{o}", align_bytes=64)
-            nc.sync.dma_start(raw[:], hT[o * P * PACK : (o + 1) * P * PACK, :].rearrange("(p j) t -> p j t", j=PACK))
-            h_raw.append(raw)
+            nc.scalar.dma_start(raw[:], hT[o * P * PACK : (o + 1) * P * PACK, :].rearrange("(p j) t -> p j t", j=PACK))
+            return raw
+
         words = []
 
         def load_words(o, tag):
@@ -70,7 +55,26 @@ def tile_picked_ysavcw_feas_p_kernel(
             nc.sync.dma_start(w[:].bitcast(I32), x_words[o].rearrange("p n r -> p (n r)").bitcast(I32))
             words.append(w)
 
+        load_col = load_column("load_col", load, nc.scalar)
+        h_raw = [load_h(0)]
+        tables = sb.tile([P, T], F32, name="tables")
+        for r, (src, queue) in enumerate(((dem, nc.sync), (depot, nc.sync), (nn, nc.scalar))):
+            queue.dma_start(tables[ROW0 + r : ROW0 + r + 1, :], src[0:1, :])
+        h_raw.append(load_h(1))
+        own_col = load_column("own_col", own, nc.sync)
         load_words(0, "words0")
+
+        planes = sb.tile([P, T], U8, name="planes", tag="planes", align_bytes=64)
+        nc.vector.memset(planes[:].bitcast(I32), 0)
+        nc.vector.memset(tables[0:ROW0, :], 0.0)
+        for q in range(4):
+            nc.sync.dma_start(
+                planes[32 * q : 32 * q + 4 * PASSES, :].bitcast(I32),
+                x_scales[:, 4 * q : 4 * q + 4, :].bitcast(I32),
+            )
+        ident = sb.tile([P, P], F32, name="ident")
+        make_identity(nc, ident[:])
+        dep2_col = load_column("dep2_col", dep2, nc.gpsimd)
 
         h_bf, h_codes, h_scales = [], [], []
         for o in range(PASSES):
@@ -89,90 +93,86 @@ def tile_picked_ysavcw_feas_p_kernel(
             h_scales.append(scales)
 
         gate_bias = sb.tile([P, ROUTE_TILES], F32, name="gate_bias")
-        nc.vector.tensor_scalar(gate_bias[:], cols["load"][:], -4.0, 4.0, ALU.mult, ALU.add)
-        root_bias = sb.tile([P, ROUTE_TILES], F32, name="root_bias")
-        nc.vector.tensor_scalar(root_bias[:], cols["own"][:], 0.36, None, ALU.mult)
-        half_dep2 = sb.tile([P, ROUTE_TILES], F32, name="half_dep2")
-        nc.vector.tensor_scalar(half_dep2[:], cols["dep2"][:], 0.5, None, ALU.mult)
+        nc.scalar.activation(gate_bias[:], load_col[:], ACT.Copy, bias=-4.0, scale=4.0)
+        dep2_scaled = sb.tile([P, ROUTE_TILES], F32, name="dep2_scaled")
+        nc.gpsimd.tensor_scalar(dep2_scaled[:], dep2_col[:], 1 / 0.6, None, ALU.mult)
 
-        picked = sb.tile([P, S], F32, name="picked")
-        nc.scalar.activation(picked[:], tables[:].indirect(offsets[:]), ACT.Copy)
-        columns = sb.tile([P, S // P, 3], F32, name="columns")
+        def spread(bank_cols, column, start, stop):
+            nc.tensor.matmul(bank_cols, column.to_broadcast([P, P]), ident[:], start=start, stop=stop, is_transpose=True)
+
+        columns = []
         for a in range(2):
-            turned = ps.tile([P, 2, P], F32, name=f"turned{a}", tag=f"acc{a}")
+            picked = sb.tile([P, HALF], F32, name=f"picked{a}")
+            nc.scalar.activation(picked[:], tables[:].indirect(offsets[:, a * HALF // 16 : (a + 1) * HALF // 16]), ACT.Copy)
+            turned = ps.tile([P, 2, P], F32, name=f"turned{a}", tag=f"acc{2 + a}")
             for i in range(2):
-                b = 2 * a + i
-                nc.tensor.transpose(turned[:, i, :], picked[:, b * P : (b + 1) * P], ident[:])
-            nc.scalar.activation(
-                columns[:, 2 * a : 2 * a + 2, :], turned[:, :, ROW0 : ROW0 + 2 * ROW_STEP + 1 : ROW_STEP], ACT.Copy, scale=0.5
-            )
-        spread = []
-        for r in range(3):
-            bank = ps.tile([P, S], F32, name=f"spread{r}", tag=f"bank{r}")
-            for b in range(S // P):
-                nc.tensor.transpose(bank[:, b * P : (b + 1) * P], columns[:, b, r : r + 1].to_broadcast([P, P]), ident[:])
-            spread.append(bank)
-        dem_rows, nn_bank, depot_rows = spread
+                nc.tensor.transpose(turned[:, i, :], picked[:, i * P : (i + 1) * P], ident[:])
+            cols = sb.tile([P, 2, 3], F32, name=f"columns{a}")
+            nc.scalar.activation(cols[:], turned[:, :, ROW0:P], ACT.Copy, scale=-1 / 0.6)
+            columns.extend(cols[:, i, :] for i in range(2))
+
+        dem_rows = ps.tile([P, S], F32, name="dem_rows", tag="acc1")
+        for b in range(BLOCKS):
+            spread(dem_rows[:, b * P : (b + 1) * P], columns[b][:, 0:1], True, True)
+        own_bank = ps.tile([P, V], F32, name="own_bank", tag="acc3")
+        for c in range(ROUTE_TILES):
+            spread(own_bank[:, c * P : (c + 1) * P], own_col[:, c : c + 1], True, True)
+        quarters = [(a, c) for a in range(2) for c in range(ROUTE_TILES)]
+        spent = {}
+        for a, c in quarters:
+            spent[a, c] = ps.tile([P, 2, P], F32, name=f"spent{a}{c}")
+            for i in range(2):
+                spread(spent[a, c][:, i, :], columns[2 * a + i][:, 1:2], i == 0, False)
         gate = []
         for c in range(ROUTE_TILES):
+            th = sb.tile([P, S], F32, name=f"tanh{c}")
+            nc.scalar.activation(th[:], dem_rows[:], ACT.Tanh, bias=gate_bias[:, c : c + 1], scale=-2.4)
             gt = sb.tile([P, S], F32, name=f"gate{c}")
-            nc.scalar.activation(gt[:], dem_rows[:], ACT.Tanh, bias=gate_bias[:, c : c + 1], scale=-8.0)
+            nc.gpsimd.tensor_scalar(gt[:], th[:], 0.3, -0.3, ALU.mult, ALU.add)
             gate.append(gt)
-        nn_rows = sb.tile([P, S], F32, name="nn_rows")
-        nc.scalar.copy(nn_rows[:], nn_bank[:])
+        own_rows = sb.tile([P, V], F32, name="own_rows")
+        nc.scalar.activation(own_rows[:], own_bank[:], ACT.Copy, scale=-1 / 0.6)
 
-        x_sc = sb.tile([P, S], U8, name="x_sc", align_bytes=64)
-        nc.vector.tensor_copy(x_sc[:], planes[:].indirect(offsets[:]))
-        x0 = sb.tile([P, S], U32, name="x0", align_bytes=64)
-        nc.vector.tensor_copy(x0[:], words[0][:].indirect(offsets[:]))
-        x1 = []
+        def gather(name, window, dtype, a, tag):
+            t = sb.tile([P, HALF], dtype, name=name, tag=tag, align_bytes=64)
+            nc.vector.tensor_copy(t[:], window[:].indirect(offsets[:, a * HALF // 16 : (a + 1) * HALF // 16]))
+            return t
+
+        x_codes, x_sc = {}, []
         for a in range(2):
-            xt = sb.tile([P, HALF], U32, name=f"x1_{a}", tag=("planes", "x1")[a], align_bytes=64)
-            nc.vector.tensor_copy(xt[:], words[1][:].indirect(offsets[:, a * HALF // 16 : (a + 1) * HALF // 16]))
-            x1.append(xt)
+            x_codes[0, a] = gather(f"x0_{a}", words[0], U32, a, f"x0_{a}")
+            x_sc.append(gather(f"x_sc{a}", planes, U8, a, f"x_sc{a}"))
+        for a in range(2):
+            x_codes[1, a] = gather(f"x1_{a}", words[1], U32, a, ("planes", "x1")[a])
 
-        quarters = [(a, c) for a in range(2) for c in range(ROUTE_TILES)]
-        acc = {}
-        for a, c in quarters:
-            acc[a, c] = ps.tile([P, HALF], F32, name=f"acc{a}{c}", tag=f"bank{c}" if a else f"acc{c}")
+        acc = [ps.tile([P, V], F32, name=f"acc{b}", tag=f"acc{b}") for b in range(BLOCKS)]
         for o in range(PASSES):
-            for a, c in quarters:
-                js = slice(a * HALF, (a + 1) * HALF)
-                ts = slice(c * P, (c + 1) * P)
-                rhs = x0[:, js] if o == 0 else x1[a][:]
+            for b in range(BLOCKS):
+                js = slice((b % 2) * P, (b % 2 + 1) * P)
                 nc.tensor.matmul_mx(
-                    out=acc[a, c][:],
-                    lhsT=h_codes[o][:, ts].bitcast(FP8X4),
-                    lhsT_scale=h_scales[o][:, ts],
-                    rhs=rhs.bitcast(FP8X4),
-                    rhs_scale=x_sc[4 * o : P, js],
+                    out=acc[b][:],
+                    lhsT=x_codes[o, b // 2][:, js].bitcast(FP8X4),
+                    lhsT_scale=x_sc[b // 2][4 * o : P, js],
+                    rhs=h_codes[o][:].bitcast(FP8X4),
+                    rhs_scale=h_scales[o][:],
                     start=(o == 0),
                     stop=(o == PASSES - 1),
                 )
 
-        root, sav = {}, {}
-
-        def distance(a, c):
-            js = slice(a * HALF, (a + 1) * HALF)
-            u = sb.tile([P, HALF], F32, name=f"u{a}{c}")
-            nc.vector.scalar_tensor_tensor(u[:], acc[a, c][:], -0.3, nn_rows[:, js], ALU.mult, ALU.add)
-            root[a, c] = sb.tile([P, HALF], F32, name=f"root{a}{c}")
-            nc.scalar.activation(root[a, c][:], u[:], ACT.Sqrt, bias=root_bias[:, c : c + 1], scale=0.72)
-
-        def saving(a, c):
-            js = slice(a * HALF, (a + 1) * HALF)
-            sav[a, c] = sb.tile([P, HALF], F32, name=f"sav{a}{c}")
-            nc.vector.scalar_tensor_tensor(
-                sav[a, c][:], depot_rows[:, js], half_dep2[:, c : c + 1], root[a, c][:], ALU.add, ALU.subtract
-            )
-
-        def result(a, c):
+        for b in range(BLOCKS):
+            u = sb.tile([P, V], F32, name=f"u{b}")
+            nc.vector.scalar_tensor_tensor(u[:], acc[b][:], columns[b][:, 2:3], own_rows[:], ALU.add, ALU.add)
+            root = sb.tile([P, V], F32, name=f"root{b}")
+            nc.scalar.activation(root[:], u[:], ACT.Sqrt, scale=-2.4)
+            for c in range(ROUTE_TILES):
+                nc.tensor.matmul(
+                    spent[b // 2, c][:, b % 2, :], root[:, c * P : (c + 1) * P], ident[:],
+                    start=False, stop=(b % 2 == 1), is_transpose=True,
+                )
+        for n, (a, c) in enumerate(quarters):
             js = slice(a * HALF, (a + 1) * HALF)
             res = sb.tile([P, HALF], F32, name=f"res{a}{c}")
-            nc.vector.scalar_tensor_tensor(res[:], gate[c][:, js], 1.0, sav[a, c][:], ALU.add, ALU.mult)
-            nc.sync.dma_start(out[c * P : (c + 1) * P, js], res[:])
-
-        for step in range(len(quarters) + 3):
-            for stage, lag in ((distance, 0), (saving, 2), (result, 3)):
-                if 0 <= step - lag < len(quarters):
-                    stage(*quarters[step - lag])
+            nc.vector.scalar_tensor_tensor(
+                res[:], spent[a, c][:].rearrange("p i j -> p (i j)"), dep2_scaled[:, c : c + 1], gate[c][:, js], ALU.subtract, ALU.mult
+            )
+            (nc.sync, nc.scalar)[n % 2].dma_start(out[c * P : (c + 1) * P, js], res[:])

from contextlib import ExitStack

import concourse.mybir as mybir
from concourse.masks import make_identity

K, T, S, V = 1024, 2048, 512, 256
FLOPS = 2 * K * S * V
BYTES = K * T + K * T // 32 + 4 * K * V + 3 * 4 * T + 3 * 4 * V + 2 * 128 * S // 16 + 4 * V * S

F32 = mybir.dt.float32
BF16 = mybir.dt.bfloat16
U32 = mybir.dt.uint32
I32 = mybir.dt.int32
U16 = mybir.dt.uint16
U8 = mybir.dt.uint8
FP8X4 = mybir.dt.float8_e4m3fn_x4
ACT = mybir.ActivationFunctionType
ALU = mybir.AluOpType

P = 128
PACK = 4
PASSES = K // (P * PACK)
ROUTE_TILES = V // P
HALF = S // 2
BLOCKS = S // P
ROW0 = P - 3


def tile_picked_ysavcw_feas_p_kernel(
    tc, x_words, x_scales, hT, nn, own, depot, dep2, dem, load, offs, out
):
    nc = tc.nc
    with ExitStack() as ctx:
        sb = ctx.enter_context(tc.tile_pool(name="sb", bufs=1))
        ps = ctx.enter_context(tc.psum_pool(name="ps", bufs=1))

        offsets = sb.tile([P, S // 16], U16, name="offsets")
        nc.sync.dma_start(offsets[:], offs)

        def load_column(name, src, queue):
            col = sb.tile([P, ROUTE_TILES], F32, name=name)
            with nc.allow_non_contiguous_dma(reason="one value a partition"):
                queue.dma_start(col[:], src.rearrange("(c p) one -> p (c one)", p=P))
            return col

        def load_h(o):
            raw = sb.tile([P, PACK, V], F32, name=f"h_raw{o}", tag=f"stage{o}", align_bytes=64)
            nc.scalar.dma_start(raw[:], hT[o * P * PACK : (o + 1) * P * PACK, :].rearrange("(p j) t -> p j t", j=PACK))
            return raw

        words = []

        def load_words(o, tag):
            w = sb.tile([P, T], U32, name=f"words{o}", tag=tag, align_bytes=64)
            nc.sync.dma_start(w[:].bitcast(I32), x_words[o].rearrange("p n r -> p (n r)").bitcast(I32))
            words.append(w)

        load_col = load_column("load_col", load, nc.scalar)
        h_raw = [load_h(0)]
        tables = sb.tile([P, T], F32, name="tables")
        for r, (src, queue) in enumerate(((dem, nc.sync), (depot, nc.sync), (nn, nc.scalar))):
            queue.dma_start(tables[ROW0 + r : ROW0 + r + 1, :], src[0:1, :])
        h_raw.append(load_h(1))
        own_col = load_column("own_col", own, nc.sync)
        load_words(0, "words0")

        planes = sb.tile([P, T], U8, name="planes", tag="planes", align_bytes=64)
        nc.vector.memset(planes[:].bitcast(I32), 0)
        nc.vector.memset(tables[0:ROW0, :], 0.0)
        for q in range(4):
            nc.sync.dma_start(
                planes[32 * q : 32 * q + 4 * PASSES, :].bitcast(I32),
                x_scales[:, 4 * q : 4 * q + 4, :].bitcast(I32),
            )
        ident = sb.tile([P, P], F32, name="ident")
        make_identity(nc, ident[:])
        dep2_col = load_column("dep2_col", dep2, nc.gpsimd)

        h_bf, h_codes, h_scales = [], [], []
        for o in range(PASSES):
            g = sb.tile([P, V, PACK], BF16, name=f"h_bf{o}", align_bytes=64)
            nc.vector.tensor_copy(
                out=g[:].rearrange("p (c i) j -> p c j i", i=4),
                in_=h_raw[o][:].rearrange("p j (c i) -> p c j i", i=4),
            )
            h_bf.append(g)
        load_words(1, "stage0")
        for o in range(PASSES):
            codes = sb.tile([P, V], U32, name=f"h_codes{o}", align_bytes=64)
            scales = sb.tile([P, V], U8, name=f"h_scales{o}", align_bytes=64)
            nc.vector.quantize_mx(out=codes[:].bitcast(FP8X4), scales=scales[:], in_=h_bf[o][:].rearrange("p t j -> p (t j)"))
            h_codes.append(codes)
            h_scales.append(scales)

        gate_bias = sb.tile([P, ROUTE_TILES], F32, name="gate_bias")
        nc.scalar.activation(gate_bias[:], load_col[:], ACT.Copy, bias=-4.0, scale=4.0)
        dep2_scaled = sb.tile([P, ROUTE_TILES], F32, name="dep2_scaled")
        nc.gpsimd.tensor_scalar(dep2_scaled[:], dep2_col[:], 1 / 0.6, None, ALU.mult)

        def spread(bank_cols, column, start, stop):
            nc.tensor.matmul(bank_cols, column.to_broadcast([P, P]), ident[:], start=start, stop=stop, is_transpose=True)

        columns = []
        for a in range(2):
            picked = sb.tile([P, HALF], F32, name=f"picked{a}")
            nc.scalar.activation(picked[:], tables[:].indirect(offsets[:, a * HALF // 16 : (a + 1) * HALF // 16]), ACT.Copy)
            turned = ps.tile([P, 2, P], F32, name=f"turned{a}", tag=f"acc{2 + a}")
            for i in range(2):
                nc.tensor.transpose(turned[:, i, :], picked[:, i * P : (i + 1) * P], ident[:])
            cols = sb.tile([P, 2, 3], F32, name=f"columns{a}")
            nc.scalar.activation(cols[:], turned[:, :, ROW0:P], ACT.Copy, scale=-1 / 0.6)
            columns.extend(cols[:, i, :] for i in range(2))

        dem_rows = ps.tile([P, S], F32, name="dem_rows", tag="acc1")
        for b in range(BLOCKS):
            spread(dem_rows[:, b * P : (b + 1) * P], columns[b][:, 0:1], True, True)
        own_bank = ps.tile([P, V], F32, name="own_bank", tag="acc3")
        for c in range(ROUTE_TILES):
            spread(own_bank[:, c * P : (c + 1) * P], own_col[:, c : c + 1], True, True)
        quarters = [(a, c) for a in range(2) for c in range(ROUTE_TILES)]
        spent = {}
        for a, c in quarters:
            spent[a, c] = ps.tile([P, 2, P], F32, name=f"spent{a}{c}")
            for i in range(2):
                spread(spent[a, c][:, i, :], columns[2 * a + i][:, 1:2], i == 0, False)
        gate = []
        for c in range(ROUTE_TILES):
            th = sb.tile([P, S], F32, name=f"tanh{c}")
            nc.scalar.activation(th[:], dem_rows[:], ACT.Tanh, bias=gate_bias[:, c : c + 1], scale=-2.4)
            gt = sb.tile([P, S], F32, name=f"gate{c}")
            nc.gpsimd.tensor_scalar(gt[:], th[:], 0.3, -0.3, ALU.mult, ALU.add)
            gate.append(gt)
        own_rows = sb.tile([P, V], F32, name="own_rows")
        nc.scalar.activation(own_rows[:], own_bank[:], ACT.Copy, scale=-1 / 0.6)

        def gather(name, window, dtype, a, tag):
            t = sb.tile([P, HALF], dtype, name=name, tag=tag, align_bytes=64)
            nc.vector.tensor_copy(t[:], window[:].indirect(offsets[:, a * HALF // 16 : (a + 1) * HALF // 16]))
            return t

        x_codes, x_sc = {}, []
        for a in range(2):
            x_codes[0, a] = gather(f"x0_{a}", words[0], U32, a, f"x0_{a}")
            x_sc.append(gather(f"x_sc{a}", planes, U8, a, f"x_sc{a}"))
        for a in range(2):
            x_codes[1, a] = gather(f"x1_{a}", words[1], U32, a, ("planes", "x1")[a])

        acc = [ps.tile([P, V], F32, name=f"acc{b}", tag=f"acc{b}") for b in range(BLOCKS)]
        for o in range(PASSES):
            for b in range(BLOCKS):
                js = slice((b % 2) * P, (b % 2 + 1) * P)
                nc.tensor.matmul_mx(
                    out=acc[b][:],
                    lhsT=x_codes[o, b // 2][:, js].bitcast(FP8X4),
                    lhsT_scale=x_sc[b // 2][4 * o : P, js],
                    rhs=h_codes[o][:].bitcast(FP8X4),
                    rhs_scale=h_scales[o][:],
                    start=(o == 0),
                    stop=(o == PASSES - 1),
                )

        for b in range(BLOCKS):
            u = sb.tile([P, V], F32, name=f"u{b}")
            nc.vector.scalar_tensor_tensor(u[:], acc[b][:], columns[b][:, 2:3], own_rows[:], ALU.add, ALU.add)
            root = sb.tile([P, V], F32, name=f"root{b}")
            nc.scalar.activation(root[:], u[:], ACT.Sqrt, scale=-2.4)
            for c in range(ROUTE_TILES):
                nc.tensor.matmul(
                    spent[b // 2, c][:, b % 2, :], root[:, c * P : (c + 1) * P], ident[:],
                    start=False, stop=(b % 2 == 1), is_transpose=True,
                )
        for n, (a, c) in enumerate(quarters):
            js = slice(a * HALF, (a + 1) * HALF)
            res = sb.tile([P, HALF], F32, name=f"res{a}{c}")
            nc.vector.scalar_tensor_tensor(
                res[:], spent[a, c][:].rearrange("p i j -> p (i j)"), dep2_scaled[:, c : c + 1], gate[c][:, js], ALU.subtract, ALU.mult
            )
            (nc.sync, nc.scalar)[n % 2].dma_start(out[c * P : (c + 1) * P, js], res[:])
